import numpy as np
import ml_dtypes


def mxq(x, axis, fmt="e4m3"):
    dtype, down = {"e4m3": (ml_dtypes.float8_e4m3fn, 7), "e5m2": (ml_dtypes.float8_e5m2, 14)}[fmt]
    v = np.moveaxis(np.asarray(x, np.float32).astype(ml_dtypes.bfloat16).astype(np.float64), axis, -1)
    blocks = v.reshape(v.shape[:-1] + (-1, 32))
    amax = np.abs(blocks).max(-1, keepdims=True)
    byte = np.maximum(np.where(amax > 0, np.frexp(amax)[1] - 1 + 127, 0) - down, 1)
    scale = np.exp2(byte - 127.0)
    codes = (blocks / scale).astype(np.float32).astype(dtype).astype(np.float64)
    return np.moveaxis((codes * scale).reshape(v.shape), -1, axis)


WIDE = False


def mx_kscale(k):
    if not WIDE:
        return np.ones(k)
    levels = np.array([10, -10, 5, -5, 0])
    if k % 512:
        return np.exp2(np.random.permutation(np.resize(levels, k // 32))).repeat(32)
    a = np.empty((k // 512, 16))
    for p in range(k // 512):
        a[p, :8] = np.random.permutation(np.resize(levels, 8))
        for g in range(8):
            far = levels[np.abs(levels - a[p, g]) >= 10]
            a[p, g + 8] = far[np.random.randint(len(far))]
    return np.exp2(a.ravel()).repeat(32)


def f64(x):
    return np.asarray(x).astype(np.float64)


def striped(idx):
    return np.tile(idx.reshape(-1, 16).T, (8, 1)).astype(np.uint16)


def unstriped(offs):
    return offs[:16].T.reshape(-1).astype(np.int64)


E2M1 = np.array([0.0, 0.5, 1.0, 1.5, 2.0, 3.0, 4.0, 6.0, -0.0, -0.5, -1.0, -1.5, -2.0, -3.0, -4.0, -6.0])


def pack_weight(w, fmt):
    k, n = w.shape
    w = f64(np.asarray(w, np.float32).astype(ml_dtypes.bfloat16)).reshape(k // 32, 32, n)
    amax = np.abs(w).max(1)
    if fmt == "e4m3":
        byte = np.frexp(amax)[1] - 1 + 127 - 7
    else:
        mant, ex = np.frexp(amax / 6.0)
        byte = np.where(mant > 0.5, ex, ex - 1) + 127
    byte = np.clip(np.where(amax > 0, byte, 1), 1, 254)
    scaled = (w * np.exp2(127.0 - byte)[:, None, :]).reshape(k, n).astype(np.float32)
    by_word = np.ascontiguousarray(scaled.reshape(k // 512, 128, 4, n).transpose(0, 1, 3, 2))
    if fmt == "e4m3":
        words = by_word.astype(ml_dtypes.float8_e4m3fn).view(np.uint8)
    else:
        c = by_word.astype(ml_dtypes.float4_e2m1fn).view(np.uint8) & 0xF
        words = (c[..., 0::2] | (c[..., 1::2] << 4)).reshape(k // 512, 128, 2 * n)
    return np.ascontiguousarray(words), np.ascontiguousarray(byte.astype(np.uint8).reshape(k // 512, 16, n))


def unpack_weight(words, scales, fmt):
    g, _, n = scales.shape
    words = np.ascontiguousarray(words).reshape(g, 128, n, -1)
    if fmt == "e4m3":
        vals = words.view(ml_dtypes.float8_e4m3fn).astype(np.float64)
    else:
        nib = np.empty((g, 128, n, 4), np.uint8)
        nib[..., 0::2] = words & 0xF
        nib[..., 1::2] = words >> 4
        vals = E2M1[nib]
    vals = vals * np.repeat(np.exp2(scales.astype(np.float64) - 127.0), 8, axis=1)[..., None]
    return vals.transpose(0, 1, 3, 2).reshape(g * 512, n)


def silu(v):
    return v / (1.0 + np.exp(-np.maximum(v, -700.0)))


K, T, E, C, H, N = 1536, 640, 2, 256, 1024, 128


def by_expert(wq, xq):
    return np.concatenate([wq[e].T @ xq[:, e * C:(e + 1) * C] for e in range(E)], axis=1)


def setup_inputs():
    n = np.random.standard_normal
    s = mx_kscale(K)[:, None]
    u = mx_kscale(H)
    w1 = [pack_weight(m, "e2m1") for m in n((E, K, H)) / np.sqrt(K) / s[None] * u[None, None, :]]
    w2 = [pack_weight(m, "e2m1") for m in n((E, H, N)) / np.sqrt(H) / u[None, :, None]]
    return {
        "xT": (n((K, T)) * s).astype(np.float32),
        "w1_words": np.stack([m[0] for m in w1]),
        "w1_scales": np.stack([m[1] for m in w1]),
        "w2_words": np.stack([m[0] for m in w2]),
        "w2_scales": np.stack([m[1] for m in w2]),
        "gate": np.tile(np.random.uniform(0.2, 1.0, E * C), (N, 1)).astype(np.float32),
        "offs": striped(np.random.permutation(T)[:E * C]),
    }


def reference(xT, w1_words, w1_scales, w2_words, w2_scales, gate, offs):
    idx = unstriped(offs)
    w1 = np.stack([unpack_weight(w1_words[e], w1_scales[e], "e2m1") for e in range(E)])
    w2 = np.stack([unpack_weight(w2_words[e], w2_scales[e], "e2m1") for e in range(E)])
    xq = mxq(f64(xT)[:, idx], 0, "e4m3")
    h = silu(by_expert(w1, xq))
    y = by_expert(w2, mxq(h, 0, "e4m3"))
    out = np.zeros((N, T))
    out[:, idx] = f64(gate) * y
    return out

@@ -1,0 +1,222 @@
+from contextlib import ExitStack
+
+import concourse.mybir as mybir
+from concourse.masks import make_identity
+
+F32 = mybir.dt.float32
+BF16 = mybir.dt.bfloat16
+I32 = mybir.dt.int32
+U32 = mybir.dt.uint32
+U16 = mybir.dt.uint16
+U8 = mybir.dt.uint8
+FP8X4 = mybir.dt.float8_e4m3fn_x4
+FP4X4 = mybir.dt.float4_e2m1fn_x4
+COPY = mybir.ActivationFunctionType.Copy
+SILU = mybir.ActivationFunctionType.Silu
+MULT = mybir.AluOpType.mult
+
+P = 128
+K, T, E, C, H, N = 1536, 640, 2, 256, 1024, 128
+KP = K // 512
+HP = H // 512
+LIST_COLS = E * C // 16
+FLOPS = 2 * E * C * (K * H + H * N)
+
+CHUNKS = (
+    (("s", 0, 256), ("v", 256, 256), ("s", 512, 128)),
+    (("s", 0, 256), ("s", 256, 256), ("v", 512, 128)),
+    (("s", 0, 256), ("s", 256, 256), ("v", 512, 128)),
+)
+ORDER = ("x0", "x1", "g00", "x2", "g01", "g10", "h02", "h11", "h12")
+
+
+def tile_moe_pln_mlp_silu_kernel(
+    tc, xT, w1_words, w1_scales, w2_words, w2_scales, gate, offs, out
+):
+    nc = tc.nc
+    with ExitStack() as ctx:
+        lists = ctx.enter_context(tc.tile_pool(name="lists", bufs=1))
+        keep = ctx.enter_context(tc.tile_pool(name="keep", bufs=1))
+        psum = ctx.enter_context(tc.psum_pool(name="psum", bufs=8))
+
+        offsets = lists.tile([P, LIST_COLS], U16, name="offsets")
+
+        warm = keep.tile([P, 1], F32, name="warm")
+        nc.vector.memset(warm[:], 0.0)
+        nc.scalar.activation(warm[:], warm[:], SILU)
+
+        w1s = keep.tile([P, E * KP * H], U8, name="w1s", align_bytes=64)
+        w2s = keep.tile([P, E * HP * N], U8, name="w2s", align_bytes=64)
+        nc.vector.memset(w1s[:].bitcast(I32), 0)
+        nc.vector.memset(w2s[:].bitcast(I32), 0)
+        xsc = []
+        for s in range(KP):
+            t = keep.tile([P, T], U8, name=f"xsc{s}", align_bytes=64)
+            nc.vector.memset(t[:].bitcast(I32), 0)
+            xsc.append(t)
+        result = keep.tile([P, T], F32, name="result")
+        nc.vector.memset(result[:], 0.0)
+
+        ident = keep.tile([P, P], F32, name="ident")
+        make_identity(nc, ident[:])
+
+        raw = {}
+        w1 = {}
+
+        def load_x(s):
+            for eng, c0, w in CHUNKS[s]:
+                t = keep.tile([P, 4, w], F32, name=f"raw{s}_{c0}")
+                nc.sync.dma_start(
+                    out=t[:], in_=xT[512 * s : 512 * (s + 1), c0 : c0 + w].rearrange("(p j) w -> p j w", j=4)
+                )
+                raw[s, c0] = t
+
+        def load_w1(e, s):
+            t = keep.tile([P, 2 * H], U8, name=f"w1_{e}_{s}", align_bytes=64)
+            nc.sync.dma_start(out=t[:].bitcast(I32), in_=w1_words[e, s].bitcast(I32))
+            w1[e, s] = t
+
+        load_x(0)
+        nc.sync.dma_start(offsets[:], offs)
+        load_x(1)
+        for q in range(4):
+            nc.sync.dma_start(
+                out=w1s[32 * q : 32 * q + 4, :].bitcast(I32).rearrange("q (e i) -> q e i", e=E * KP),
+                in_=w1_scales[:, :, 4 * q : 4 * q + 4, :].bitcast(I32).rearrange("e s q i -> q (e s) i"),
+            )
+        load_w1(0, 0)
+        load_x(2)
+        load_w1(0, 1)
+        load_w1(1, 0)
+        load_w1(1, 1)
+        load_w1(0, 2)
+        load_w1(1, 2)
+        w2 = keep.tile([P, E * HP, 2 * N], U8, name="w2", align_bytes=64)
+        nc.sync.dma_start(
+            out=w2[:].rearrange("p e b -> p (e b)").bitcast(I32).rearrange("p (e b) -> p e b", e=E * HP),
+            in_=w2_words.bitcast(I32).rearrange("e s p b -> p (e s) b"),
+        )
+        for q in range(4):
+            nc.sync.dma_start(
+                out=w2s[32 * q : 32 * q + 4, :].bitcast(I32).rearrange("q (e i) -> q e i", e=E * HP),
+                in_=w2_scales[:, :, 4 * q : 4 * q + 4, :].bitcast(I32).rearrange("e s q i -> q (e s) i"),
+            )
+        gates = keep.tile([P, E * C], F32, name="gates")
+        nc.sync.dma_start(out=gates[:], in_=gate)
+
+        xw = [keep.tile([P, T], U32, name=f"xw{s}", align_bytes=64) for s in range(KP)]
+        gw, gs, acc = {}, {}, {}
+
+        def quantise_x(s):
+            mixed = []
+            for eng, c0, w in CHUNKS[s]:
+                src = raw[s, c0][:].rearrange("p j w -> p w j")
+                t = keep.tile([P, w, 4], BF16, name=f"xb{s}_{c0}", align_bytes=64)
+                if eng == "s":
+                    nc.scalar.activation(t[:], src, COPY)
+                else:
+                    nc.vector.tensor_copy(t[:], src)
+                mixed.append((t, c0, w))
+            for t, c0, w in mixed:
+                nc.vector.quantize_mx(
+                    out=xw[s][:, c0 : c0 + w].bitcast(FP8X4),
+                    scales=xsc[s][:, c0 : c0 + w],
+                    in_=t[:].rearrange("p w j -> p (w j)"),
+                )
+
+        def gather(e, s, parts):
+            a = keep.tile([P, C], U32, name=f"gw{e}_{s}", align_bytes=64)
+            b = keep.tile([P, C], U8, name=f"gs{e}_{s}", align_bytes=64)
+            n = C // parts
+            for h in range(parts):
+                o = (e * C + h * n) // 16
+                idx = offsets[:, o : o + n // 16]
+                nc.vector.tensor_copy(a[:, h * n : (h + 1) * n], xw[s][:].indirect(idx))
+                nc.vector.tensor_copy(b[:, h * n : (h + 1) * n], xsc[s][:].indirect(idx))
+            gw[e, s], gs[e, s] = a, b
+
+        def first_layer(e, s):
+            for half in range(2):
+                st = 2 * e + half
+                cols = slice(half * P, (half + 1) * P)
+                for g in range(HP):
+                    if s == 0:
+                        acc[st, g] = psum.tile([P, 512], F32, name=f"acc{st}_{g}", tag="bank")
+                    wcol = (e * KP + s) * H + g * 512
+                    nc.tensor.matmul_mx(
+                        out=acc[st, g][:],
+                        lhsT=gw[e, s][:, cols].bitcast(FP8X4),
+                        lhsT_scale=gs[e, s][:, cols],
+                        rhs=w1[e, s][:, g * 1024 : (g + 1) * 1024].bitcast(FP4X4),
+                        rhs_scale=w1s[:, wcol : wcol + 512],
+                        start=(s == 0),
+                        stop=(s == KP - 1),
+                    )
+
+        tps = {}
+
+        def hidden(st):
+            hs = keep.tile([P, H], BF16, name=f"hs{st}", align_bytes=64)
+            words = hs[:].bitcast(F32)
+            for g in range(HP):
+                nc.scalar.activation(
+                    hs[:, g * 512 : (g + 1) * 512].rearrange("p (u m d) -> p u m d", u=2, d=2),
+                    acc[st, g][:].rearrange("p (m u d) -> p u m d", u=2, d=2),
+                    SILU,
+                )
+            for g in range(HP):
+                tp = psum.tile([P, 512], F32, name=f"tp{st}_{g}", tag="bank")
+                for u in range(2):
+                    b = 2 * g + u
+                    nc.tensor.transpose(tp[:, u * P : (u + 1) * P], words[:, b * P : (b + 1) * P], ident[:])
+                tps[st, g] = tp
+
+        ys = {}
+
+        def second_layer(st):
+            e = st // 2
+            y = psum.tile([P, 512], F32, name=f"y{st}", tag="bank")
+            hb = keep.tile([P, HP, 512], BF16, name=f"hb{st}", align_bytes=64)
+            hw = keep.tile([P, HP, P], U32, name=f"hw{st}", align_bytes=64)
+            hc = keep.tile([P, HP, P], U8, name=f"hc{st}", align_bytes=64)
+            for g in range(HP):
+                dst = hb[:, g, :].bitcast(F32).rearrange("p (r u) -> p r u", u=2)
+                src = tps[st, g][:, 0 : 2 * P].rearrange("p (u r) -> p r u", u=2)
+                if st >= 2:
+                    nc.scalar.copy(dst, src)
+                else:
+                    nc.vector.tensor_copy(dst, src)
+            for g in range(HP):
+                nc.vector.quantize_mx(out=hw[:, g, :].bitcast(FP8X4), scales=hc[:, g, :], in_=hb[:, g, :])
+            for g in range(HP):
+                row = e * HP + g
+                nc.tensor.matmul_mx(
+                    out=y[:, 0:P],
+                    lhsT=w2[:, row, :].bitcast(FP4X4),
+                    lhsT_scale=w2s[:, row * N : (row + 1) * N],
+                    rhs=hw[:, g, :].bitcast(FP8X4),
+                    rhs_scale=hc[:, g, :],
+                    start=(g == 0),
+                    stop=(g == HP - 1),
+                )
+            yt = keep.tile([P, P], F32, name=f"yt{st}")
+            nc.scalar.copy(yt[:], y[:, 0:P])
+            ys[st] = yt
+
+        for step in ORDER:
+            if step[0] == "x":
+                quantise_x(int(step[1]))
+            else:
+                e, s = int(step[1]), int(step[2])
+                gather(e, s, 2 if step[0] == "h" else 1)
+                first_layer(e, s)
+        for st in range(2 * E):
+            hidden(st)
+        for st in range(2 * E):
+            second_layer(st)
+        for st in range(2 * E):
+            nc.vector.tensor_tensor(
+                result[:].indirect(offsets[:, st * 8 : (st + 1) * 8]), ys[st][:], gates[:, st * P : (st + 1) * P], MULT
+            )
+
+        nc.sync.dma_start(out=out, in_=result[:])

@@ -22,12 +22,15 @@ HP = H // 512
 LIST_COLS = E * C // 16
 FLOPS = 2 * E * C * (K * H + H * N)
 
+LOADS = (((0, 640),), ((0, 640),), ((0, 256), (256, 384)))
 CHUNKS = (
+    (("s", 0, 256), ("v", 256, 384)),
     (("s", 0, 256), ("v", 256, 256), ("s", 512, 128)),
-    (("s", 0, 256), ("s", 256, 256), ("v", 512, 128)),
-    (("s", 0, 256), ("s", 256, 256), ("v", 512, 128)),
+    (("s", 0, 512), ("v", 512, 128)),
 )
-ORDER = ("x0", "x1", "g00", "x2", "g01", "g10", "h02", "h11", "h12")
+QUANTS = ((0, 512), (512, 128))
+ORDER = ("x0", "x1", "g10", "g00", "x2", "h01", "h02", "h11", "h12")
+CP = "VSVV"
 
 
 def tile_moe_pln_mlp_silu_kernel(
@@ -60,11 +63,17 @@ def tile_moe_pln_mlp_silu_kernel(
         ident = keep.tile([P, P], F32, name="ident")
         make_identity(nc, ident[:])
 
+        for q in range(4):
+            nc.gpsimd.dma_start(
+                out=w1s[32 * q : 32 * q + 4, :].bitcast(I32).rearrange("q (e i) -> q e i", e=E * KP),
+                in_=w1_scales[:, :, 4 * q : 4 * q + 4, :].bitcast(I32).rearrange("e s q i -> q (e s) i"),
+            )
+
         raw = {}
         w1 = {}
 
         def load_x(s):
-            for eng, c0, w in CHUNKS[s]:
+            for c0, w in LOADS[s]:
                 t = keep.tile([P, 4, w], F32, name=f"raw{s}_{c0}")
                 nc.sync.dma_start(
                     out=t[:], in_=xT[512 * s : 512 * (s + 1), c0 : c0 + w].rearrange("(p j) w -> p j w", j=4)
@@ -79,15 +88,10 @@ def tile_moe_pln_mlp_silu_kernel(
         load_x(0)
         nc.sync.dma_start(offsets[:], offs)
         load_x(1)
-        for q in range(4):
-            nc.sync.dma_start(
-                out=w1s[32 * q : 32 * q + 4, :].bitcast(I32).rearrange("q (e i) -> q e i", e=E * KP),
-                in_=w1_scales[:, :, 4 * q : 4 * q + 4, :].bitcast(I32).rearrange("e s q i -> q (e s) i"),
-            )
-        load_w1(0, 0)
-        load_x(2)
-        load_w1(0, 1)
         load_w1(1, 0)
+        load_x(2)
+        load_w1(0, 0)
+        load_w1(0, 1)
         load_w1(1, 1)
         load_w1(0, 2)
         load_w1(1, 2)
@@ -106,22 +110,26 @@ def tile_moe_pln_mlp_silu_kernel(
 
         xw = [keep.tile([P, T], U32, name=f"xw{s}", align_bytes=64) for s in range(KP)]
         gw, gs, acc = {}, {}, {}
+        for st in range(2 * E):
+            for g in range(HP):
+                acc[st, g] = psum.tile([P, 512], F32, name=f"acc{st}_{g}", tag="bank")
 
         def quantise_x(s):
-            mixed = []
+            mixed = keep.tile([P, T, 4], BF16, name=f"xb{s}", align_bytes=64)
             for eng, c0, w in CHUNKS[s]:
-                src = raw[s, c0][:].rearrange("p j w -> p w j")
-                t = keep.tile([P, w, 4], BF16, name=f"xb{s}_{c0}", align_bytes=64)
-                if eng == "s":
-                    nc.scalar.activation(t[:], src, COPY)
-                else:
-                    nc.vector.tensor_copy(t[:], src)
-                mixed.append((t, c0, w))
-            for t, c0, w in mixed:
+                for l0, lw in LOADS[s]:
+                    lo, hi = max(c0, l0), min(c0 + w, l0 + lw)
+                    if lo < hi:
+                        src = raw[s, l0][:, :, lo - l0 : hi - l0].rearrange("p j w -> p w j")
+                        if eng == "s":
+                            nc.scalar.activation(mixed[:, lo:hi, :], src, COPY)
+                        else:
+                            nc.vector.tensor_copy(mixed[:, lo:hi, :], src)
+            for c0, w in QUANTS:
                 nc.vector.quantize_mx(
                     out=xw[s][:, c0 : c0 + w].bitcast(FP8X4),
                     scales=xsc[s][:, c0 : c0 + w],
-                    in_=t[:].rearrange("p w j -> p (w j)"),
+                    in_=mixed[:, c0 : c0 + w, :].rearrange("p w j -> p (w j)"),
                 )
 
         def gather(e, s, parts):
@@ -140,8 +148,6 @@ def tile_moe_pln_mlp_silu_kernel(
                 st = 2 * e + half
                 cols = slice(half * P, (half + 1) * P)
                 for g in range(HP):
-                    if s == 0:
-                        acc[st, g] = psum.tile([P, 512], F32, name=f"acc{st}_{g}", tag="bank")
                     wcol = (e * KP + s) * H + g * 512
                     nc.tensor.matmul_mx(
                         out=acc[st, g][:],
@@ -182,7 +188,7 @@ def tile_moe_pln_mlp_silu_kernel(
             for g in range(HP):
                 dst = hb[:, g, :].bitcast(F32).rearrange("p (r u) -> p r u", u=2)
                 src = tps[st, g][:, 0 : 2 * P].rearrange("p (u r) -> p r u", u=2)
-                if st >= 2:
+                if CP[st] == "S":
                     nc.scalar.copy(dst, src)
                 else:
                     nc.vector.tensor_copy(dst, src)

@@ -22,15 +22,14 @@ HP = H // 512
 LIST_COLS = E * C // 16
 FLOPS = 2 * E * C * (K * H + H * N)
 
-LOADS = (((0, 640),), ((0, 640),), ((0, 256), (256, 384)))
 CHUNKS = (
     (("s", 0, 256), ("v", 256, 384)),
-    (("s", 0, 256), ("v", 256, 256), ("s", 512, 128)),
-    (("s", 0, 512), ("v", 512, 128)),
+    (("v", 0, 256), ("s", 256, 384)),
+    (("v", 0, 256), ("s", 256, 384)),
 )
 QUANTS = ((0, 512), (512, 128))
-ORDER = ("x0", "x1", "g10", "g00", "x2", "h01", "h02", "h11", "h12")
-CP = "VSVV"
+ORDER = ("x0", "g00", "x1", "g01", "x2", "h10", "h02", "h11", "h12")
+TURN = ("vv", "vv", "vs", "ss")
 
 
 def tile_moe_pln_mlp_silu_kernel(
@@ -63,22 +62,24 @@ def tile_moe_pln_mlp_silu_kernel(
         ident = keep.tile([P, P], F32, name="ident")
         make_identity(nc, ident[:])
 
-        for q in range(4):
-            nc.gpsimd.dma_start(
-                out=w1s[32 * q : 32 * q + 4, :].bitcast(I32).rearrange("q (e i) -> q e i", e=E * KP),
-                in_=w1_scales[:, :, 4 * q : 4 * q + 4, :].bitcast(I32).rearrange("e s q i -> q (e s) i"),
-            )
 
         raw = {}
         w1 = {}
 
         def load_x(s):
-            for c0, w in LOADS[s]:
-                t = keep.tile([P, 4, w], F32, name=f"raw{s}_{c0}")
+            raw[s] = keep.tile([P, 4, T], F32, name=f"raw{s}")
+            nc.sync.dma_start(
+                out=raw[s][:], in_=xT[512 * s : 512 * (s + 1), :].rearrange("(p j) w -> p j w", j=4)
+            )
+
+        def load_w1_scales(e):
+            for q in range(4):
                 nc.sync.dma_start(
-                    out=t[:], in_=xT[512 * s : 512 * (s + 1), c0 : c0 + w].rearrange("(p j) w -> p j w", j=4)
+                    out=w1s[32 * q : 32 * q + 4, e * KP * H : (e + 1) * KP * H]
+                    .bitcast(I32)
+                    .rearrange("q (s i) -> q s i", s=KP),
+                    in_=w1_scales[e, :, 4 * q : 4 * q + 4, :].bitcast(I32).rearrange("s q i -> q s i"),
                 )
-                raw[s, c0] = t
 
         def load_w1(e, s):
             t = keep.tile([P, 2 * H], U8, name=f"w1_{e}_{s}", align_bytes=64)
@@ -88,13 +89,15 @@ def tile_moe_pln_mlp_silu_kernel(
         load_x(0)
         nc.sync.dma_start(offsets[:], offs)
         load_x(1)
-        load_w1(1, 0)
-        load_x(2)
+        load_w1_scales(0)
         load_w1(0, 0)
+        load_x(2)
+        load_w1(1, 0)
         load_w1(0, 1)
-        load_w1(1, 1)
+        load_w1_scales(1)
         load_w1(0, 2)
         load_w1(1, 2)
+        load_w1(1, 1)
         w2 = keep.tile([P, E * HP, 2 * N], U8, name="w2", align_bytes=64)
         nc.sync.dma_start(
             out=w2[:].rearrange("p e b -> p (e b)").bitcast(I32).rearrange("p (e b) -> p e b", e=E * HP),
@@ -117,14 +120,11 @@ def tile_moe_pln_mlp_silu_kernel(
         def quantise_x(s):
             mixed = keep.tile([P, T, 4], BF16, name=f"xb{s}", align_bytes=64)
             for eng, c0, w in CHUNKS[s]:
-                for l0, lw in LOADS[s]:
-                    lo, hi = max(c0, l0), min(c0 + w, l0 + lw)
-                    if lo < hi:
-                        src = raw[s, l0][:, :, lo - l0 : hi - l0].rearrange("p j w -> p w j")
-                        if eng == "s":
-                            nc.scalar.activation(mixed[:, lo:hi, :], src, COPY)
-                        else:
-                            nc.vector.tensor_copy(mixed[:, lo:hi, :], src)
+                src = raw[s][:, :, c0 : c0 + w].rearrange("p j w -> p w j")
+                if eng == "s":
+                    nc.scalar.activation(mixed[:, c0 : c0 + w, :], src, COPY)
+                else:
+                    nc.vector.tensor_copy(mixed[:, c0 : c0 + w, :], src)
             for c0, w in QUANTS:
                 nc.vector.quantize_mx(
                     out=xw[s][:, c0 : c0 + w].bitcast(FP8X4),
@@ -188,7 +188,7 @@ def tile_moe_pln_mlp_silu_kernel(
             for g in range(HP):
                 dst = hb[:, g, :].bitcast(F32).rearrange("p (r u) -> p r u", u=2)
                 src = tps[st, g][:, 0 : 2 * P].rearrange("p (u r) -> p r u", u=2)
-                if CP[st] == "S":
+                if TURN[st][g] == "s":
                     nc.scalar.copy(dst, src)
                 else:
                     nc.vector.tensor_copy(dst, src)
@@ -218,7 +218,6 @@ def tile_moe_pln_mlp_silu_kernel(
                 first_layer(e, s)
         for st in range(2 * E):
             hidden(st)
-        for st in range(2 * E):
             second_layer(st)
         for st in range(2 * E):
             nc.vector.tensor_tensor(

@@ -24,12 +24,11 @@ FLOPS = 2 * E * C * (K * H + H * N)
 
 CHUNKS = (
     (("s", 0, 256), ("v", 256, 384)),
-    (("v", 0, 256), ("s", 256, 384)),
-    (("v", 0, 256), ("s", 256, 384)),
+    (("s", 0, 640),),
+    (("s", 0, 512), ("v", 512, 128)),
 )
 QUANTS = ((0, 512), (512, 128))
-ORDER = ("x0", "g00", "x1", "g01", "x2", "h10", "h02", "h11", "h12")
-TURN = ("vv", "vv", "vs", "ss")
+TURN = ("vv", "vv", "sv", "ss")
 
 
 def tile_moe_pln_mlp_silu_kernel(
@@ -39,7 +38,7 @@ def tile_moe_pln_mlp_silu_kernel(
     with ExitStack() as ctx:
         lists = ctx.enter_context(tc.tile_pool(name="lists", bufs=1))
         keep = ctx.enter_context(tc.tile_pool(name="keep", bufs=1))
-        psum = ctx.enter_context(tc.psum_pool(name="psum", bufs=8))
+        psum = ctx.enter_context(tc.psum_pool(name="psum", bufs=1))
 
         offsets = lists.tile([P, LIST_COLS], U16, name="offsets")
 
@@ -47,9 +46,10 @@ def tile_moe_pln_mlp_silu_kernel(
         nc.vector.memset(warm[:], 0.0)
         nc.scalar.activation(warm[:], warm[:], SILU)
 
-        w1s = keep.tile([P, E * KP * H], U8, name="w1s", align_bytes=64)
+        w1s = [keep.tile([P, KP * H], U8, name=f"w1s{e}", align_bytes=64) for e in range(E)]
         w2s = keep.tile([P, E * HP * N], U8, name="w2s", align_bytes=64)
-        nc.vector.memset(w1s[:].bitcast(I32), 0)
+        for e in range(E):
+            nc.vector.memset(w1s[e][:].bitcast(I32), 0)
         nc.vector.memset(w2s[:].bitcast(I32), 0)
         xsc = []
         for s in range(KP):
@@ -73,12 +73,10 @@ def tile_moe_pln_mlp_silu_kernel(
             )
 
         def load_w1_scales(e):
-            for q in range(4):
+            for r in range(4):
                 nc.sync.dma_start(
-                    out=w1s[32 * q : 32 * q + 4, e * KP * H : (e + 1) * KP * H]
-                    .bitcast(I32)
-                    .rearrange("q (s i) -> q s i", s=KP),
-                    in_=w1_scales[e, :, 4 * q : 4 * q + 4, :].bitcast(I32).rearrange("s q i -> q s i"),
+                    out=w1s[e][r:P:32, :].bitcast(I32).rearrange("q (s i) -> q s i", s=KP),
+                    in_=w1_scales[e, :, r:16:4, :].bitcast(I32).rearrange("s q i -> q s i"),
                 )
 
         def load_w1(e, s):
@@ -89,15 +87,15 @@ def tile_moe_pln_mlp_silu_kernel(
         load_x(0)
         nc.sync.dma_start(offsets[:], offs)
         load_x(1)
-        load_w1_scales(0)
-        load_w1(0, 0)
         load_x(2)
-        load_w1(1, 0)
-        load_w1(0, 1)
-        load_w1_scales(1)
-        load_w1(0, 2)
-        load_w1(1, 2)
-        load_w1(1, 1)
+        for e in range(E):
+            load_w1_scales(e)
+            if e == 0:
+                load_w1(0, 0)
+                load_w1(1, 0)
+        for s in range(1, KP):
+            for e in range(E):
+                load_w1(e, s)
         w2 = keep.tile([P, E * HP, 2 * N], U8, name="w2", align_bytes=64)
         nc.sync.dma_start(
             out=w2[:].rearrange("p e b -> p (e b)").bitcast(I32).rearrange("p (e b) -> p e b", e=E * HP),
@@ -115,16 +113,17 @@ def tile_moe_pln_mlp_silu_kernel(
         gw, gs, acc = {}, {}, {}
         for st in range(2 * E):
             for g in range(HP):
-                acc[st, g] = psum.tile([P, 512], F32, name=f"acc{st}_{g}", tag="bank")
+                acc[st, g] = psum.tile([P, 512], F32, name=f"acc{st}_{g}", tag=f"bank{2 * st + g}")
 
         def quantise_x(s):
             mixed = keep.tile([P, T, 4], BF16, name=f"xb{s}", align_bytes=64)
             for eng, c0, w in CHUNKS[s]:
-                src = raw[s][:, :, c0 : c0 + w].rearrange("p j w -> p w j")
+                src = raw[s][:, :, c0 : c0 + w].rearrange("p j (c i) -> p c j i", i=4)
+                dst = mixed[:, c0 : c0 + w, :].rearrange("p (c i) j -> p c j i", i=4)
                 if eng == "s":
-                    nc.scalar.activation(mixed[:, c0 : c0 + w, :], src, COPY)
+                    nc.scalar.activation(dst, src, COPY)
                 else:
-                    nc.vector.tensor_copy(mixed[:, c0 : c0 + w, :], src)
+                    nc.vector.tensor_copy(dst, src)
             for c0, w in QUANTS:
                 nc.vector.quantize_mx(
                     out=xw[s][:, c0 : c0 + w].bitcast(FP8X4),
@@ -132,32 +131,31 @@ def tile_moe_pln_mlp_silu_kernel(
                     in_=mixed[:, c0 : c0 + w, :].rearrange("p w j -> p (w j)"),
                 )
 
-        def gather(e, s, parts):
-            a = keep.tile([P, C], U32, name=f"gw{e}_{s}", align_bytes=64)
-            b = keep.tile([P, C], U8, name=f"gs{e}_{s}", align_bytes=64)
-            n = C // parts
-            for h in range(parts):
-                o = (e * C + h * n) // 16
-                idx = offsets[:, o : o + n // 16]
-                nc.vector.tensor_copy(a[:, h * n : (h + 1) * n], xw[s][:].indirect(idx))
-                nc.vector.tensor_copy(b[:, h * n : (h + 1) * n], xsc[s][:].indirect(idx))
-            gw[e, s], gs[e, s] = a, b
+        for e in range(E):
+            for s in range(KP):
+                gw[e, s] = keep.tile([P, C], U32, name=f"gw{e}_{s}", align_bytes=64)
+                gs[e, s] = keep.tile([P, C], U8, name=f"gs{e}_{s}", align_bytes=64)
 
-        def first_layer(e, s):
-            for half in range(2):
-                st = 2 * e + half
-                cols = slice(half * P, (half + 1) * P)
-                for g in range(HP):
-                    wcol = (e * KP + s) * H + g * 512
-                    nc.tensor.matmul_mx(
-                        out=acc[st, g][:],
-                        lhsT=gw[e, s][:, cols].bitcast(FP8X4),
-                        lhsT_scale=gs[e, s][:, cols],
-                        rhs=w1[e, s][:, g * 1024 : (g + 1) * 1024].bitcast(FP4X4),
-                        rhs_scale=w1s[:, wcol : wcol + 512],
-                        start=(s == 0),
-                        stop=(s == KP - 1),
-                    )
+        def gather(e, s, lo, n):
+            o = (e * C + lo) // 16
+            idx = offsets[:, o : o + n // 16]
+            nc.vector.tensor_copy(gw[e, s][:, lo : lo + n], xw[s][:].indirect(idx))
+            nc.vector.tensor_copy(gs[e, s][:, lo : lo + n], xsc[s][:].indirect(idx))
+
+        def first_layer(e, s, half):
+            st = 2 * e + half
+            cols = slice(half * P, (half + 1) * P)
+            for g in range(HP):
+                wcol = s * H + g * 512
+                nc.tensor.matmul_mx(
+                    out=acc[st, g][:],
+                    lhsT=gw[e, s][:, cols].bitcast(FP8X4),
+                    lhsT_scale=gs[e, s][:, cols],
+                    rhs=w1[e, s][:, g * 1024 : (g + 1) * 1024].bitcast(FP4X4),
+                    rhs_scale=w1s[e][:, wcol : wcol + 512],
+                    start=(s == 0),
+                    stop=(s == KP - 1),
+                )
 
         tps = {}
 
@@ -171,7 +169,7 @@ def tile_moe_pln_mlp_silu_kernel(
                     SILU,
                 )
             for g in range(HP):
-                tp = psum.tile([P, 512], F32, name=f"tp{st}_{g}", tag="bank")
+                tp = psum.tile([P, 512], F32, name=f"tp{st}_{g}", tag=f"bank{2 * st + g}")
                 for u in range(2):
                     b = 2 * g + u
                     nc.tensor.transpose(tp[:, u * P : (u + 1) * P], words[:, b * P : (b + 1) * P], ident[:])
@@ -181,7 +179,7 @@ def tile_moe_pln_mlp_silu_kernel(
 
         def second_layer(st):
             e = st // 2
-            y = psum.tile([P, 512], F32, name=f"y{st}", tag="bank")
+            y = psum.tile([P, 512], F32, name=f"y{st}", tag=f"bank{2 * st}")
             hb = keep.tile([P, HP, 512], BF16, name=f"hb{st}", align_bytes=64)
             hw = keep.tile([P, HP, P], U32, name=f"hw{st}", align_bytes=64)
             hc = keep.tile([P, HP, P], U8, name=f"hc{st}", align_bytes=64)
@@ -192,8 +190,11 @@ def tile_moe_pln_mlp_silu_kernel(
                     nc.scalar.copy(dst, src)
                 else:
                     nc.vector.tensor_copy(dst, src)
-            for g in range(HP):
-                nc.vector.quantize_mx(out=hw[:, g, :].bitcast(FP8X4), scales=hc[:, g, :], in_=hb[:, g, :])
+            nc.vector.quantize_mx(
+                out=hw[:].rearrange("p g r -> p (g r)").bitcast(FP8X4),
+                scales=hc[:].rearrange("p g r -> p (g r)"),
+                in_=hb[:].rearrange("p g c -> p (g c)"),
+            )
             for g in range(HP):
                 row = e * HP + g
                 nc.tensor.matmul_mx(
@@ -209,13 +210,28 @@ def tile_moe_pln_mlp_silu_kernel(
             nc.scalar.copy(yt[:], y[:, 0:P])
             ys[st] = yt
 
-        for step in ORDER:
-            if step[0] == "x":
-                quantise_x(int(step[1]))
-            else:
-                e, s = int(step[1]), int(step[2])
-                gather(e, s, 2 if step[0] == "h" else 1)
-                first_layer(e, s)
+        def both(e, s):
+            gather(e, s, 0, C)
+            for half in range(2):
+                first_layer(e, s, half)
+
+        def one(e, s, half):
+            gather(e, s, half * P, P)
+            first_layer(e, s, half)
+
+        quantise_x(0)
+        both(0, 0)
+        quantise_x(1)
+        quantise_x(2)
+        one(1, 0, 0)
+        one(1, 0, 1)
+        both(0, 1)
+        one(0, 2, 0)
+        one(1, 1, 0)
+        one(0, 2, 1)
+        one(1, 2, 0)
+        one(1, 1, 1)
+        one(1, 2, 1)
         for st in range(2 * E):
             hidden(st)
             second_layer(st)

from contextlib import ExitStack

import concourse.mybir as mybir
from concourse.masks import make_identity

F32 = mybir.dt.float32
BF16 = mybir.dt.bfloat16
I32 = mybir.dt.int32
U32 = mybir.dt.uint32
U16 = mybir.dt.uint16
U8 = mybir.dt.uint8
FP8X4 = mybir.dt.float8_e4m3fn_x4
FP4X4 = mybir.dt.float4_e2m1fn_x4
COPY = mybir.ActivationFunctionType.Copy
SILU = mybir.ActivationFunctionType.Silu
MULT = mybir.AluOpType.mult

P = 128
K, T, E, C, H, N = 1536, 640, 2, 256, 1024, 128
KP = K // 512
HP = H // 512
LIST_COLS = E * C // 16
FLOPS = 2 * E * C * (K * H + H * N)

CHUNKS = (
    (("s", 0, 256), ("v", 256, 384)),
    (("s", 0, 640),),
    (("s", 0, 512), ("v", 512, 128)),
)
QUANTS = ((0, 512), (512, 128))
TURN = ("vv", "vv", "sv", "ss")


def tile_moe_pln_mlp_silu_kernel(
    tc, xT, w1_words, w1_scales, w2_words, w2_scales, gate, offs, out
):
    nc = tc.nc
    with ExitStack() as ctx:
        lists = ctx.enter_context(tc.tile_pool(name="lists", bufs=1))
        keep = ctx.enter_context(tc.tile_pool(name="keep", bufs=1))
        psum = ctx.enter_context(tc.psum_pool(name="psum", bufs=1))

        offsets = lists.tile([P, LIST_COLS], U16, name="offsets")

        warm = keep.tile([P, 1], F32, name="warm")
        nc.vector.memset(warm[:], 0.0)
        nc.scalar.activation(warm[:], warm[:], SILU)

        w1s = [keep.tile([P, KP * H], U8, name=f"w1s{e}", align_bytes=64) for e in range(E)]
        w2s = keep.tile([P, E * HP * N], U8, name="w2s", align_bytes=64)
        for e in range(E):
            nc.vector.memset(w1s[e][:].bitcast(I32), 0)
        nc.vector.memset(w2s[:].bitcast(I32), 0)
        xsc = []
        for s in range(KP):
            t = keep.tile([P, T], U8, name=f"xsc{s}", align_bytes=64)
            nc.vector.memset(t[:].bitcast(I32), 0)
            xsc.append(t)
        result = keep.tile([P, T], F32, name="result")
        nc.vector.memset(result[:], 0.0)

        ident = keep.tile([P, P], F32, name="ident")
        make_identity(nc, ident[:])


        raw = {}
        w1 = {}

        def load_x(s):
            raw[s] = keep.tile([P, 4, T], F32, name=f"raw{s}")
            nc.sync.dma_start(
                out=raw[s][:], in_=xT[512 * s : 512 * (s + 1), :].rearrange("(p j) w -> p j w", j=4)
            )

        def load_w1_scales(e):
            for r in range(4):
                nc.sync.dma_start(
                    out=w1s[e][r:P:32, :].bitcast(I32).rearrange("q (s i) -> q s i", s=KP),
                    in_=w1_scales[e, :, r:16:4, :].bitcast(I32).rearrange("s q i -> q s i"),
                )

        def load_w1(e, s):
            t = keep.tile([P, 2 * H], U8, name=f"w1_{e}_{s}", align_bytes=64)
            nc.sync.dma_start(out=t[:].bitcast(I32), in_=w1_words[e, s].bitcast(I32))
            w1[e, s] = t

        load_x(0)
        nc.sync.dma_start(offsets[:], offs)
        load_x(1)
        load_x(2)
        for e in range(E):
            load_w1_scales(e)
            if e == 0:
                load_w1(0, 0)
                load_w1(1, 0)
        for s in range(1, KP):
            for e in range(E):
                load_w1(e, s)
        w2 = keep.tile([P, E * HP, 2 * N], U8, name="w2", align_bytes=64)
        nc.sync.dma_start(
            out=w2[:].rearrange("p e b -> p (e b)").bitcast(I32).rearrange("p (e b) -> p e b", e=E * HP),
            in_=w2_words.bitcast(I32).rearrange("e s p b -> p (e s) b"),
        )
        for q in range(4):
            nc.sync.dma_start(
                out=w2s[32 * q : 32 * q + 4, :].bitcast(I32).rearrange("q (e i) -> q e i", e=E * HP),
                in_=w2_scales[:, :, 4 * q : 4 * q + 4, :].bitcast(I32).rearrange("e s q i -> q (e s) i"),
            )
        gates = keep.tile([P, E * C], F32, name="gates")
        nc.sync.dma_start(out=gates[:], in_=gate)

        xw = [keep.tile([P, T], U32, name=f"xw{s}", align_bytes=64) for s in range(KP)]
        gw, gs, acc = {}, {}, {}
        for st in range(2 * E):
            for g in range(HP):
                acc[st, g] = psum.tile([P, 512], F32, name=f"acc{st}_{g}", tag=f"bank{2 * st + g}")

        def quantise_x(s):
            mixed = keep.tile([P, T, 4], BF16, name=f"xb{s}", align_bytes=64)
            for eng, c0, w in CHUNKS[s]:
                src = raw[s][:, :, c0 : c0 + w].rearrange("p j (c i) -> p c j i", i=4)
                dst = mixed[:, c0 : c0 + w, :].rearrange("p (c i) j -> p c j i", i=4)
                if eng == "s":
                    nc.scalar.activation(dst, src, COPY)
                else:
                    nc.vector.tensor_copy(dst, src)
            for c0, w in QUANTS:
                nc.vector.quantize_mx(
                    out=xw[s][:, c0 : c0 + w].bitcast(FP8X4),
                    scales=xsc[s][:, c0 : c0 + w],
                    in_=mixed[:, c0 : c0 + w, :].rearrange("p w j -> p (w j)"),
                )

        for e in range(E):
            for s in range(KP):
                gw[e, s] = keep.tile([P, C], U32, name=f"gw{e}_{s}", align_bytes=64)
                gs[e, s] = keep.tile([P, C], U8, name=f"gs{e}_{s}", align_bytes=64)

        def gather(e, s, lo, n):
            o = (e * C + lo) // 16
            idx = offsets[:, o : o + n // 16]
            nc.vector.tensor_copy(gw[e, s][:, lo : lo + n], xw[s][:].indirect(idx))
            nc.vector.tensor_copy(gs[e, s][:, lo : lo + n], xsc[s][:].indirect(idx))

        def first_layer(e, s, half):
            st = 2 * e + half
            cols = slice(half * P, (half + 1) * P)
            for g in range(HP):
                wcol = s * H + g * 512
                nc.tensor.matmul_mx(
                    out=acc[st, g][:],
                    lhsT=gw[e, s][:, cols].bitcast(FP8X4),
                    lhsT_scale=gs[e, s][:, cols],
                    rhs=w1[e, s][:, g * 1024 : (g + 1) * 1024].bitcast(FP4X4),
                    rhs_scale=w1s[e][:, wcol : wcol + 512],
                    start=(s == 0),
                    stop=(s == KP - 1),
                )

        tps = {}

        def hidden(st):
            hs = keep.tile([P, H], BF16, name=f"hs{st}", align_bytes=64)
            words = hs[:].bitcast(F32)
            for g in range(HP):
                nc.scalar.activation(
                    hs[:, g * 512 : (g + 1) * 512].rearrange("p (u m d) -> p u m d", u=2, d=2),
                    acc[st, g][:].rearrange("p (m u d) -> p u m d", u=2, d=2),
                    SILU,
                )
            for g in range(HP):
                tp = psum.tile([P, 512], F32, name=f"tp{st}_{g}", tag=f"bank{2 * st + g}")
                for u in range(2):
                    b = 2 * g + u
                    nc.tensor.transpose(tp[:, u * P : (u + 1) * P], words[:, b * P : (b + 1) * P], ident[:])
                tps[st, g] = tp

        ys = {}

        def second_layer(st):
            e = st // 2
            y = psum.tile([P, 512], F32, name=f"y{st}", tag=f"bank{2 * st}")
            hb = keep.tile([P, HP, 512], BF16, name=f"hb{st}", align_bytes=64)
            hw = keep.tile([P, HP, P], U32, name=f"hw{st}", align_bytes=64)
            hc = keep.tile([P, HP, P], U8, name=f"hc{st}", align_bytes=64)
            for g in range(HP):
                dst = hb[:, g, :].bitcast(F32).rearrange("p (r u) -> p r u", u=2)
                src = tps[st, g][:, 0 : 2 * P].rearrange("p (u r) -> p r u", u=2)
                if TURN[st][g] == "s":
                    nc.scalar.copy(dst, src)
                else:
                    nc.vector.tensor_copy(dst, src)
            nc.vector.quantize_mx(
                out=hw[:].rearrange("p g r -> p (g r)").bitcast(FP8X4),
                scales=hc[:].rearrange("p g r -> p (g r)"),
                in_=hb[:].rearrange("p g c -> p (g c)"),
            )
            for g in range(HP):
                row = e * HP + g
                nc.tensor.matmul_mx(
                    out=y[:, 0:P],
                    lhsT=w2[:, row, :].bitcast(FP4X4),
                    lhsT_scale=w2s[:, row * N : (row + 1) * N],
                    rhs=hw[:, g, :].bitcast(FP8X4),
                    rhs_scale=hc[:, g, :],
                    start=(g == 0),
                    stop=(g == HP - 1),
                )
            yt = keep.tile([P, P], F32, name=f"yt{st}")
            nc.scalar.copy(yt[:], y[:, 0:P])
            ys[st] = yt

        def both(e, s):
            gather(e, s, 0, C)
            for half in range(2):
                first_layer(e, s, half)

        def one(e, s, half):
            gather(e, s, half * P, P)
            first_layer(e, s, half)

        quantise_x(0)
        both(0, 0)
        quantise_x(1)
        quantise_x(2)
        one(1, 0, 0)
        one(1, 0, 1)
        both(0, 1)
        one(0, 2, 0)
        one(1, 1, 0)
        one(0, 2, 1)
        one(1, 2, 0)
        one(1, 1, 1)
        one(1, 2, 1)
        for st in range(2 * E):
            hidden(st)
            second_layer(st)
        for st in range(2 * E):
            nc.vector.tensor_tensor(
                result[:].indirect(offsets[:, st * 8 : (st + 1) * 8]), ys[st][:], gates[:, st * P : (st + 1) * P], MULT
            )

        nc.sync.dma_start(out=out, in_=result[:])
